import numpy as np
import ml_dtypes


def mxq(x, axis, fmt="e4m3"):
    dtype, down = {"e4m3": (ml_dtypes.float8_e4m3fn, 7), "e5m2": (ml_dtypes.float8_e5m2, 14)}[fmt]
    v = np.moveaxis(np.asarray(x, np.float32).astype(ml_dtypes.bfloat16).astype(np.float64), axis, -1)
    blocks = v.reshape(v.shape[:-1] + (-1, 32))
    amax = np.abs(blocks).max(-1, keepdims=True)
    byte = np.maximum(np.where(amax > 0, np.frexp(amax)[1] - 1 + 127, 0) - down, 1)
    scale = np.exp2(byte - 127.0)
    codes = (blocks / scale).astype(np.float32).astype(dtype).astype(np.float64)
    return np.moveaxis((codes * scale).reshape(v.shape), -1, axis)


WIDE = False


def mx_kscale(k):
    if not WIDE:
        return np.ones(k)
    levels = np.array([10, -10, 5, -5, 0])
    if k % 512:
        return np.exp2(np.random.permutation(np.resize(levels, k // 32))).repeat(32)
    a = np.empty((k // 512, 16))
    for p in range(k // 512):
        a[p, :8] = np.random.permutation(np.resize(levels, 8))
        for g in range(8):
            far = levels[np.abs(levels - a[p, g]) >= 10]
            a[p, g + 8] = far[np.random.randint(len(far))]
    return np.exp2(a.ravel()).repeat(32)


def f64(x):
    return np.asarray(x).astype(np.float64)


def striped(idx):
    return np.tile(np.asarray(idx).reshape(-1, 16).T, (8, 1)).astype(np.uint16)


def unstriped(offs):
    return offs[:16].T.reshape(-1).astype(np.int64)


def sigmoid(v):
    return 1.0 / (1.0 + np.exp(-v))


D, T, I, Q, E, U, M = 512, 2048, 512, 256, 512, 1024, 1024


def setup_inputs():
    n = np.random.standard_normal
    idx = np.random.permutation(T)[:I]
    idx2 = np.random.permutation(U)[:I]
    idx3 = np.random.permutation(M)[:Q]
    fd = mx_kscale(D)
    fi = mx_kscale(I)
    ti = np.ones(T)
    ti[idx] = fi
    return {
        "query": (n((D, Q)) * 0.9 / np.sqrt(D) * fd[:, None]).astype(np.float32),
        "keys": (n((D, T)) / fd[:, None]).astype(np.float32),
        "notes": (n((D, U)) / fd[:, None]).astype(np.float32),
        "os": (np.random.uniform(0.02, 0.08, (1, I)) * fi).astype(np.float32),
        "vals": (n((E, T)) / ti).astype(np.float32),
        "old": (n((E, M)) * 2.0).astype(np.float32),
        "fade": (np.random.uniform(0.3, 0.9, (1, M))).astype(np.float32),
        "offs": striped(idx),
        "offs2": striped(idx2),
        "offs3": striped(idx3),
    }


def reference(query, keys, notes, os, vals, old, fade, offs, offs2, offs3):
    idx = unstriped(offs)
    idx2 = unstriped(offs2)
    idx3 = unstriped(offs3)
    zk = np.maximum(f64(keys)[:, idx], f64(notes)[:, idx2])
    queryq = mxq(f64(query), 0, "e4m3")
    zkq = mxq(zk, 0, "e4m3")
    s = queryq.T @ zkq
    w = sigmoid(s)
    wo1 = w * f64(os)
    wt1 = wo1.T
    vt1 = f64(vals)[:, idx].T
    vt1q = mxq(vt1, 0, "e4m3")
    wt1q = mxq(wt1, 0, "e4m3")
    o = vt1q.T @ wt1q
    of = np.zeros((E, M))
    of[:, idx3] = o
    y = f64(old) * f64(fade) + of
    return y

@@ -1,0 +1,244 @@
+from contextlib import ExitStack
+
+import concourse.mybir as mybir
+from concourse.masks import make_identity
+
+D, T, I, Q, E, U, M = 512, 2048, 512, 256, 512, 1024, 1024
+FLOPS = 2 * D * I * Q + 2 * I * E * Q
+
+F32 = mybir.dt.float32
+BF16 = mybir.dt.bfloat16
+U32 = mybir.dt.uint32
+U16 = mybir.dt.uint16
+U8 = mybir.dt.uint8
+FP8X4 = mybir.dt.float8_e4m3fn_x4
+ALU = mybir.AluOpType
+ACT = mybir.ActivationFunctionType
+
+P = 128
+PACK = 4
+BANK = 512
+
+
+def tile_attend_keylarger_written_lean_kernel(tc, query, keys, notes, slot_factor, vals, old, fade, offs, offs2, offs3, out):
+    nc = tc.nc
+    with ExitStack() as ctx:
+        sb = ctx.enter_context(tc.tile_pool(name="sb", bufs=1))
+        ps = ctx.enter_context(tc.psum_pool(name="ps", bufs=1))
+
+        def tile(shape, dtype, name, after=None):
+            return sb.tile(shape, dtype, name=name, tag=after or name, align_bytes=64)
+
+        key_list = tile([P, I // 16], U16, "key_list")
+        note_list = tile([P, I // 16], U16, "note_list")
+        place_list = tile([P, Q // 16], U16, "place_list")
+        key_rows = keys.rearrange("(p j) t -> p j t", j=PACK)
+        note_rows = notes.rearrange("(p j) u -> p j u", j=PACK)
+        key_pool = [tile([P, T], F32, "key_pool%d" % j) for j in range(PACK)]
+        note_pool = [tile([P, U], F32, "note_pool%d" % j) for j in range(PACK)]
+        val_pool = [tile([P, T], F32, "val_pool%d" % k) for k in range(4)]
+        old_sb = [tile([P, M], F32, "old_sb%d" % k) for k in range(4)]
+        query_sb = tile([P, PACK, Q], F32, "query_sb")
+        factor_sb = tile([P, PACK], F32, "factor_sb")
+        fade_sb = tile([P, 2, PACK], F32, "fade_sb")
+
+        def load_vals(k):
+            nc.sync.dma_start(out=val_pool[k][:], in_=vals[k * P:(k + 1) * P, :])
+
+        def load_old(k):
+            nc.sync.dma_start(out=old_sb[k][:], in_=old[k * P:(k + 1) * P, :])
+
+        nc.sync.dma_start(out=key_pool[0][:], in_=key_rows[:, 0, :])
+        nc.sync.dma_start(key_list[:], offs)
+        nc.sync.dma_start(note_list[:], offs2)
+        nc.sync.dma_start(out=note_pool[0][:], in_=note_rows[:, 0, :])
+        nc.sync.dma_start(out=factor_sb[:], in_=slot_factor.rearrange("o (p t) -> p (o t)", t=PACK))
+        nc.sync.dma_start(out=fade_sb[:], in_=fade.rearrange("o (h p c) -> p (o h) c", h=2, c=PACK))
+        for j in range(1, PACK):
+            nc.sync.dma_start(out=key_pool[j][:], in_=key_rows[:, j, :])
+            nc.sync.dma_start(out=note_pool[j][:], in_=note_rows[:, j, :])
+        nc.sync.dma_start(out=query_sb[:], in_=query.rearrange("(p j) q -> p j q", j=PACK))
+        nc.sync.dma_start(place_list[:], offs3)
+        load_vals(0)
+        load_vals(1)
+        load_old(0)
+        load_vals(2)
+        load_old(1)
+        load_vals(3)
+        load_old(2)
+        load_old(3)
+
+        ident = tile([P, P], F32, "ident")
+        make_identity(nc, ident[:])
+
+        fade_all = [ps.tile([P, PACK, P], F32, name="fade_all%d" % h) for h in range(2)]
+        for h in range(2):
+            for c in range(PACK):
+                nc.tensor.transpose(fade_all[h][:, c, :], fade_sb[:, h, c:c + 1].to_broadcast([P, P]), ident[:])
+
+        placed = [tile([P, M], F32, "placed%d" % k) for k in range(4)]
+        for k in range(4):
+            nc.vector.memset(placed[k][:], 0.0)
+
+        zk_rows = tile([P, PACK, I], BF16, "zk_rows")
+        last = PACK - 1
+        half = I // 2
+        for j in range(last):
+            key_got = tile([P, I], F32, "key_got%d" % j)
+            note_got = tile([P, I], F32, "note_got%d" % j)
+            nc.vector.tensor_copy(key_got[:], key_pool[j][:].indirect(key_list[:]))
+            nc.scalar.activation(note_got[:], note_pool[j][:].indirect(note_list[:]), ACT.Copy)
+            nc.vector.tensor_tensor(zk_rows[:, j, :], key_got[:], note_got[:], ALU.max)
+        key_got = tile([P, I], F32, "key_got3")
+        nc.vector.tensor_copy(key_got[:], key_pool[last][:].indirect(key_list[:]))
+        note_low = tile([P, half], F32, "note_low", after="key_pool3")
+        note_high = tile([P, half], F32, "note_high", after="note_pool2")
+        nc.vector.tensor_copy(note_low[:], note_pool[last][:].indirect(note_list[:, :half // 16]))
+        nc.scalar.activation(note_high[:], note_pool[last][:].indirect(note_list[:, half // 16:]), ACT.Copy)
+        nc.vector.tensor_tensor(zk_rows[:, last, :half], key_got[:, :half], note_low[:], ALU.max)
+        nc.vector.tensor_tensor(zk_rows[:, last, half:], key_got[:, half:], note_high[:], ALU.max)
+
+        query_bf = tile([P, Q, PACK], BF16, "query_bf", after="note_pool3")
+        nc.scalar.copy(
+            out=query_bf[:].rearrange("p (c i) j -> p c j i", i=4),
+            in_=query_sb[:].rearrange("p j (c i) -> p c j i", i=4),
+        )
+        query_codes = tile([P, Q], U32, "query_codes")
+        query_scales = tile([P, Q], U8, "query_scales")
+
+        zk_dealt = zk_rows[:].rearrange("p j (m t) -> p t m j", t=PACK)
+        zk_bf = [tile([P, 2 * P, PACK], BF16, "zk_bf%d" % g, after=[None, "query_sb"][g]) for g in range(2)]
+        zk_codes = [tile([P, 2 * P], U32, "zk_codes%d" % g, after=[None, "note_pool3"][g]) for g in range(2)]
+        zk_scales = [tile([P, 2 * P], U8, "zk_scales%d" % g) for g in range(2)]
+        scores = [ps.tile([P, PACK, P], F32, name="scores%d" % h) for h in range(2)]
+
+        def quantize(codes, scales, values):
+            nc.vector.quantize_mx(
+                out=codes[:].bitcast(FP8X4), scales=scales[:], in_=values[:].rearrange("p c j -> p (c j)")
+            )
+
+        def score(g):
+            quantize(zk_codes[g], zk_scales[g], zk_bf[g])
+            for h in range(2):
+                rows = slice(h * P, (h + 1) * P)
+                for r in range(2):
+                    slots = slice(r * P, (r + 1) * P)
+                    nc.tensor.matmul_mx(
+                        out=scores[h][:, 2 * g + r, :],
+                        lhsT=zk_codes[g][:, slots].bitcast(FP8X4),
+                        lhsT_scale=zk_scales[g][:, slots],
+                        rhs=query_codes[:, rows].bitcast(FP8X4),
+                        rhs_scale=query_scales[:, rows],
+                        start=True,
+                        stop=True,
+                    )
+
+        for r in range(2):
+            nc.vector.tensor_copy(zk_bf[0][:, r * P:(r + 1) * P, :], zk_dealt[:, r])
+        for r in range(2):
+            nc.scalar.copy(out=zk_bf[1][:, r * P:(r + 1) * P, :], in_=zk_dealt[:, 2 + r])
+        quantize(query_codes, query_scales, query_bf)
+        score(0)
+        score(1)
+
+        got, val_bf, val_codes, val_scales, read_sb, faded = {}, {}, {}, {}, {}, {}
+
+        def gather_vals(k, on_vector, after):
+            got[k] = tile([P, I], BF16, "val_got%d" % k, after=after)
+            looked_up = val_pool[k][:].indirect(key_list[:])
+            if on_vector:
+                nc.vector.tensor_copy(got[k][:], looked_up)
+            else:
+                nc.scalar.activation(got[k][:], looked_up, ACT.Copy)
+
+        def turn_vals(k, bank):
+            words = got[k][:].bitcast(F32)
+            turned = ps.tile([P, 2, P], F32, name="turned%d" % k, tag=bank)
+            for u in range(2):
+                nc.tensor.transpose(turned[:, u, :], words[:, u:I // 2:2], ident[:])
+            val_bf[k] = tile([P, P, PACK], BF16, "val_bf%d" % k)
+            nc.scalar.copy(out=val_bf[k][:].bitcast(F32), in_=turned[:].rearrange("p u e -> p e u"))
+
+        def quantize_vals(k, after):
+            val_codes[k] = tile([P, P], U32, "val_codes%d" % k, after=after)
+            val_scales[k] = tile([P, P], U8, "val_scales%d" % k)
+            quantize(val_codes[k], val_scales[k], val_bf[k])
+
+        gather_vals(0, True, "query_sb")
+
+        weight_bf = tile([P, Q, PACK], BF16, "weight_bf", after="val_pool0")
+        weight_codes = tile([P, Q], U32, "weight_codes")
+        weight_scales = tile([P, Q], U8, "weight_scales")
+        for h in range(2):
+            weight = tile([P, P, PACK], F32, "weight%d" % h)
+            nc.scalar.activation(weight[:], scores[h][:].rearrange("p t q -> p q t"), ACT.Sigmoid)
+            nc.vector.tensor_tensor(
+                weight_bf[:, h * P:(h + 1) * P, :],
+                weight[:],
+                factor_sb[:].unsqueeze(1).to_broadcast([P, P, PACK]),
+                ALU.mult,
+            )
+
+        def read_vals(k, after=None):
+            read = ps.tile([P, Q], F32, name="read%d" % k, tag="read%d" % (k % 2))
+            nc.tensor.matmul_mx(
+                out=read[:],
+                lhsT=val_codes[k][:].bitcast(FP8X4),
+                lhsT_scale=val_scales[k][:],
+                rhs=weight_codes[:].bitcast(FP8X4),
+                rhs_scale=weight_scales[:],
+                start=True,
+                stop=True,
+            )
+            read_sb[k] = tile([P, Q], F32, "read_sb%d" % k, after=after)
+            nc.scalar.copy(out=read_sb[k][:], in_=read[:])
+
+        def place(k):
+            nc.scalar.activation(placed[k][:].indirect(place_list[:]), read_sb[k][:], ACT.Copy)
+
+        def fade_old(k, after):
+            faded[k] = tile([P, M], F32, "faded%d" % k, after=after)
+            for h in range(2):
+                cols = slice(h * BANK, (h + 1) * BANK)
+                nc.vector.tensor_tensor(
+                    faded[k][:, cols].rearrange("p (n c) -> p n c", c=PACK),
+                    old_sb[k][:, cols].rearrange("p (n c) -> p n c", c=PACK),
+                    fade_all[h][:].rearrange("p c n -> p n c"),
+                    ALU.mult,
+                )
+
+        def add_and_store(k, after, pieces=1):
+            result = tile([P, M], F32, "result%d" % k, after=after)
+            for n in range(pieces):
+                cols = slice(n * M // pieces, (n + 1) * M // pieces)
+                nc.vector.tensor_tensor(result[:, cols], faded[k][:, cols], placed[k][:, cols], ALU.add)
+                nc.sync.dma_start(out=out[k * P:(k + 1) * P, cols], in_=result[:, cols])
+
+        turn_vals(0, "scores0")
+        quantize_vals(0, "weight1")
+        quantize(weight_codes, weight_scales, weight_bf)
+        gather_vals(1, False, "query_sb")
+        turn_vals(1, "turned_a")
+        read_vals(0, "query_sb")
+        place(0)
+        fade_old(0, "val_pool0")
+        quantize_vals(1, "old_sb0")
+        gather_vals(2, True, "val_bf1")
+        turn_vals(2, "turned_b")
+        gather_vals(3, False, "val_bf1")
+        read_vals(1, "val_pool3")
+        place(1)
+        fade_old(1, "val_pool2")
+        quantize_vals(2, "old_sb1")
+        turn_vals(3, "turned_a")
+        read_vals(2, "val_pool3")
+        place(2)
+        add_and_store(0, "val_bf2")
+        fade_old(2, "val_pool0")
+        quantize_vals(3, "old_sb2")
+        read_vals(3, "val_pool3")
+        place(3)
+        add_and_store(1, "val_bf3")
+        fade_old(3, "val_pool2")
+        add_and_store(2, "old_sb3")
+        add_and_store(3, None, pieces=2)

@@ -52,51 +52,71 @@ def tile_attend_keylarger_written_lean_kernel(tc, query, keys, notes, slot_facto
         nc.sync.dma_start(key_list[:], offs)
         nc.sync.dma_start(note_list[:], offs2)
         nc.sync.dma_start(out=note_pool[0][:], in_=note_rows[:, 0, :])
-        nc.sync.dma_start(out=factor_sb[:], in_=slot_factor.rearrange("o (p t) -> p (o t)", t=PACK))
-        nc.sync.dma_start(out=fade_sb[:], in_=fade.rearrange("o (h p c) -> p (o h) c", h=2, c=PACK))
+        nc.scalar.dma_start(out=factor_sb[:], in_=slot_factor.rearrange("o (p t) -> p (o t)", t=PACK))
+        nc.scalar.dma_start(out=fade_sb[:], in_=fade.rearrange("o (h p c) -> p (o h) c", h=2, c=PACK))
         for j in range(1, PACK):
             nc.sync.dma_start(out=key_pool[j][:], in_=key_rows[:, j, :])
             nc.sync.dma_start(out=note_pool[j][:], in_=note_rows[:, j, :])
         nc.sync.dma_start(out=query_sb[:], in_=query.rearrange("(p j) q -> p j q", j=PACK))
-        nc.sync.dma_start(place_list[:], offs3)
         load_vals(0)
-        load_vals(1)
         load_old(0)
-        load_vals(2)
+        load_vals(1)
+        nc.sync.dma_start(place_list[:], offs3)
         load_old(1)
+        load_vals(2)
         load_vals(3)
         load_old(2)
         load_old(3)
 
+        zero = tile([P, 1], F32, "zero")
+        unread = tile([P, 1], F32, "unread")
+        nc.vector.memset(zero[:], 0.0)
+        nc.scalar.activation(unread[:], zero[:], ACT.Sigmoid)
+
         ident = tile([P, P], F32, "ident")
         make_identity(nc, ident[:])
 
-        fade_all = [ps.tile([P, PACK, P], F32, name="fade_all%d" % h) for h in range(2)]
+        fade_all = tile([P, M], F32, "fade_all")
         for h in range(2):
+            fade_bank = ps.tile([P, PACK, P], F32, name="fade_bank%d" % h)
             for c in range(PACK):
-                nc.tensor.transpose(fade_all[h][:, c, :], fade_sb[:, h, c:c + 1].to_broadcast([P, P]), ident[:])
+                nc.tensor.transpose(fade_bank[:, c, :], fade_sb[:, h, c:c + 1].to_broadcast([P, P]), ident[:])
+            nc.scalar.copy(
+                out=fade_all[:, h * BANK:(h + 1) * BANK].rearrange("p (n c) -> p n c", c=PACK),
+                in_=fade_bank[:].rearrange("p c n -> p n c"),
+            )
 
         placed = [tile([P, M], F32, "placed%d" % k) for k in range(4)]
         for k in range(4):
             nc.vector.memset(placed[k][:], 0.0)
 
         zk_rows = tile([P, PACK, I], BF16, "zk_rows")
+        zk_places = zk_rows[:].rearrange("p j (t m) -> p j m t", t=PACK)
+
+        def larger(j, slots, key_got, note_got):
+            nc.vector.tensor_tensor(
+                zk_places[:, j, slots.start // PACK:slots.stop // PACK, :],
+                key_got.rearrange("p (m t) -> p m t", t=PACK),
+                note_got.rearrange("p (m t) -> p m t", t=PACK),
+                ALU.max,
+            )
+
         last = PACK - 1
         half = I // 2
         for j in range(last):
             key_got = tile([P, I], F32, "key_got%d" % j)
             note_got = tile([P, I], F32, "note_got%d" % j)
-            nc.vector.tensor_copy(key_got[:], key_pool[j][:].indirect(key_list[:]))
-            nc.scalar.activation(note_got[:], note_pool[j][:].indirect(note_list[:]), ACT.Copy)
-            nc.vector.tensor_tensor(zk_rows[:, j, :], key_got[:], note_got[:], ALU.max)
+            nc.scalar.activation(key_got[:], key_pool[j][:].indirect(key_list[:]), ACT.Copy)
+            nc.vector.tensor_copy(note_got[:], note_pool[j][:].indirect(note_list[:]))
+            larger(j, slice(0, I), key_got[:], note_got[:])
         key_got = tile([P, I], F32, "key_got3")
-        nc.vector.tensor_copy(key_got[:], key_pool[last][:].indirect(key_list[:]))
-        note_low = tile([P, half], F32, "note_low", after="key_pool3")
-        note_high = tile([P, half], F32, "note_high", after="note_pool2")
+        nc.scalar.activation(key_got[:], key_pool[last][:].indirect(key_list[:]), ACT.Copy)
+        note_low = tile([P, half], F32, "note_low")
+        note_high = tile([P, half], F32, "note_high", after="key_pool3")
         nc.vector.tensor_copy(note_low[:], note_pool[last][:].indirect(note_list[:, :half // 16]))
         nc.scalar.activation(note_high[:], note_pool[last][:].indirect(note_list[:, half // 16:]), ACT.Copy)
-        nc.vector.tensor_tensor(zk_rows[:, last, :half], key_got[:, :half], note_low[:], ALU.max)
-        nc.vector.tensor_tensor(zk_rows[:, last, half:], key_got[:, half:], note_high[:], ALU.max)
+        larger(last, slice(0, half), key_got[:, :half], note_low[:])
+        larger(last, slice(half, I), key_got[:, half:], note_high[:])
 
         query_bf = tile([P, Q, PACK], BF16, "query_bf", after="note_pool3")
         nc.scalar.copy(
@@ -106,19 +126,18 @@ def tile_attend_keylarger_written_lean_kernel(tc, query, keys, notes, slot_facto
         query_codes = tile([P, Q], U32, "query_codes")
         query_scales = tile([P, Q], U8, "query_scales")
 
-        zk_dealt = zk_rows[:].rearrange("p j (m t) -> p t m j", t=PACK)
-        zk_bf = [tile([P, 2 * P, PACK], BF16, "zk_bf%d" % g, after=[None, "query_sb"][g]) for g in range(2)]
+        zk_bf = tile([P, I, PACK], BF16, "zk_bf")
         zk_codes = [tile([P, 2 * P], U32, "zk_codes%d" % g, after=[None, "note_pool3"][g]) for g in range(2)]
         zk_scales = [tile([P, 2 * P], U8, "zk_scales%d" % g) for g in range(2)]
         scores = [ps.tile([P, PACK, P], F32, name="scores%d" % h) for h in range(2)]
 
         def quantize(codes, scales, values):
             nc.vector.quantize_mx(
-                out=codes[:].bitcast(FP8X4), scales=scales[:], in_=values[:].rearrange("p c j -> p (c j)")
+                out=codes[:].bitcast(FP8X4), scales=scales[:], in_=values.rearrange("p c j -> p (c j)")
             )
 
         def score(g):
-            quantize(zk_codes[g], zk_scales[g], zk_bf[g])
+            quantize(zk_codes[g], zk_scales[g], zk_bf[:, 2 * P * g:2 * P * (g + 1), :])
             for h in range(2):
                 rows = slice(h * P, (h + 1) * P)
                 for r in range(2):
@@ -133,11 +152,13 @@ def tile_attend_keylarger_written_lean_kernel(tc, query, keys, notes, slot_facto
                         stop=True,
                     )
 
-        for r in range(2):
-            nc.vector.tensor_copy(zk_bf[0][:, r * P:(r + 1) * P, :], zk_dealt[:, r])
-        for r in range(2):
-            nc.scalar.copy(out=zk_bf[1][:, r * P:(r + 1) * P, :], in_=zk_dealt[:, 2 + r])
-        quantize(query_codes, query_scales, query_bf)
+        for g in range(2):
+            cols = slice(2 * P * g, 2 * P * (g + 1))
+            nc.vector.tensor_copy(
+                zk_bf[:, cols, :].rearrange("p (c i) j -> p c j i", i=4),
+                zk_rows[:, :, cols].rearrange("p j (c i) -> p c j i", i=4),
+            )
+        quantize(query_codes, query_scales, query_bf[:])
         score(0)
         score(1)
 
@@ -151,35 +172,26 @@ def tile_attend_keylarger_written_lean_kernel(tc, query, keys, notes, slot_facto
             else:
                 nc.scalar.activation(got[k][:], looked_up, ACT.Copy)
 
-        def turn_vals(k, bank):
+        def turn_vals(k, on_vector, after):
             words = got[k][:].bitcast(F32)
-            turned = ps.tile([P, 2, P], F32, name="turned%d" % k, tag=bank)
+            turned = ps.tile([P, 2, P], F32, name="turned%d" % k, tag="turned%d" % (k % 2))
             for u in range(2):
                 nc.tensor.transpose(turned[:, u, :], words[:, u:I // 2:2], ident[:])
-            val_bf[k] = tile([P, P, PACK], BF16, "val_bf%d" % k)
-            nc.scalar.copy(out=val_bf[k][:].bitcast(F32), in_=turned[:].rearrange("p u e -> p e u"))
+            val_bf[k] = tile([P, P, PACK], BF16, "val_bf%d" % k, after=after)
+            if on_vector:
+                nc.vector.tensor_copy(val_bf[k][:].bitcast(F32), turned[:].rearrange("p u e -> p e u"))
+            else:
+                nc.scalar.copy(out=val_bf[k][:].bitcast(F32), in_=turned[:].rearrange("p u e -> p e u"))
 
         def quantize_vals(k, after):
             val_codes[k] = tile([P, P], U32, "val_codes%d" % k, after=after)
             val_scales[k] = tile([P, P], U8, "val_scales%d" % k)
-            quantize(val_codes[k], val_scales[k], val_bf[k])
+            quantize(val_codes[k], val_scales[k], val_bf[k][:])
 
-        gather_vals(0, True, "query_sb")
-
-        weight_bf = tile([P, Q, PACK], BF16, "weight_bf", after="val_pool0")
         weight_codes = tile([P, Q], U32, "weight_codes")
         weight_scales = tile([P, Q], U8, "weight_scales")
-        for h in range(2):
-            weight = tile([P, P, PACK], F32, "weight%d" % h)
-            nc.scalar.activation(weight[:], scores[h][:].rearrange("p t q -> p q t"), ACT.Sigmoid)
-            nc.vector.tensor_tensor(
-                weight_bf[:, h * P:(h + 1) * P, :],
-                weight[:],
-                factor_sb[:].unsqueeze(1).to_broadcast([P, P, PACK]),
-                ALU.mult,
-            )
 
-        def read_vals(k, after=None):
+        def read_vals(k, on_vector, after):
             read = ps.tile([P, Q], F32, name="read%d" % k, tag="read%d" % (k % 2))
             nc.tensor.matmul_mx(
                 out=read[:],
@@ -191,54 +203,62 @@ def tile_attend_keylarger_written_lean_kernel(tc, query, keys, notes, slot_facto
                 stop=True,
             )
             read_sb[k] = tile([P, Q], F32, "read_sb%d" % k, after=after)
-            nc.scalar.copy(out=read_sb[k][:], in_=read[:])
+            if on_vector:
+                nc.vector.tensor_copy(read_sb[k][:], read[:])
+            else:
+                nc.scalar.copy(out=read_sb[k][:], in_=read[:])
 
         def place(k):
             nc.scalar.activation(placed[k][:].indirect(place_list[:]), read_sb[k][:], ACT.Copy)
 
         def fade_old(k, after):
             faded[k] = tile([P, M], F32, "faded%d" % k, after=after)
-            for h in range(2):
-                cols = slice(h * BANK, (h + 1) * BANK)
-                nc.vector.tensor_tensor(
-                    faded[k][:, cols].rearrange("p (n c) -> p n c", c=PACK),
-                    old_sb[k][:, cols].rearrange("p (n c) -> p n c", c=PACK),
-                    fade_all[h][:].rearrange("p c n -> p n c"),
-                    ALU.mult,
-                )
+            nc.vector.tensor_tensor(faded[k][:], old_sb[k][:], fade_all[:], ALU.mult)
 
-        def add_and_store(k, after, pieces=1):
-            result = tile([P, M], F32, "result%d" % k, after=after)
+        def add_and_store(k, result, pieces=1):
             for n in range(pieces):
                 cols = slice(n * M // pieces, (n + 1) * M // pieces)
                 nc.vector.tensor_tensor(result[:, cols], faded[k][:, cols], placed[k][:, cols], ALU.add)
                 nc.sync.dma_start(out=out[k * P:(k + 1) * P, cols], in_=result[:, cols])
 
-        turn_vals(0, "scores0")
-        quantize_vals(0, "weight1")
-        quantize(weight_codes, weight_scales, weight_bf)
+        gather_vals(0, False, "query_sb")
+        fade_old(0, "zk_bf")
+        weight_bf = tile([P, Q, PACK], BF16, "weight_bf", after="old_sb0")
+        weight = tile([P, Q, PACK], F32, "weight", after="val_pool0")
+        for h in range(2):
+            rows = slice(h * P, (h + 1) * P)
+            nc.scalar.activation(weight[:, rows, :], scores[h][:].rearrange("p t q -> p q t"), ACT.Sigmoid)
+            nc.vector.tensor_tensor(
+                weight_bf[:, rows, :],
+                weight[:, rows, :],
+                factor_sb[:].unsqueeze(1).to_broadcast([P, P, PACK]),
+                ALU.mult,
+            )
+        turn_vals(0, False, None)
+        quantize_vals(0, "val_pool0")
+        quantize(weight_codes, weight_scales, weight_bf[:])
         gather_vals(1, False, "query_sb")
-        turn_vals(1, "turned_a")
-        read_vals(0, "query_sb")
+        read_vals(0, False, "val_pool1")
         place(0)
-        fade_old(0, "val_pool0")
-        quantize_vals(1, "old_sb0")
-        gather_vals(2, True, "val_bf1")
-        turn_vals(2, "turned_b")
-        gather_vals(3, False, "val_bf1")
-        read_vals(1, "val_pool3")
+        fade_old(1, "val_bf0")
+        turn_vals(1, True, "old_sb1")
+        quantize_vals(1, None)
+        gather_vals(2, True, None)
+        gather_vals(3, False, "val_pool1")
+        read_vals(1, False, "val_pool3")
         place(1)
-        fade_old(1, "val_pool2")
-        quantize_vals(2, "old_sb1")
-        turn_vals(3, "turned_a")
-        read_vals(2, "val_pool3")
+        add_and_store(0, tile([P, M], F32, "result0", after="val_pool2"))
+        turn_vals(2, True, None)
+        quantize_vals(2, None)
+        read_vals(2, False, "val_pool3")
         place(2)
-        add_and_store(0, "val_bf2")
-        fade_old(2, "val_pool0")
-        quantize_vals(3, "old_sb2")
-        read_vals(3, "val_pool3")
+        fade_old(2, None)
+        turn_vals(3, True, "old_sb2")
+        quantize_vals(3, None)
+        add_and_store(1, tile([P, M], F32, "result1", after="old_sb2"))
+        read_vals(3, True, None)
         place(3)
-        add_and_store(1, "val_bf3")
-        fade_old(3, "val_pool2")
-        add_and_store(2, "old_sb3")
-        add_and_store(3, None, pieces=2)
+        fade_old(3, "val_bf0")
+        last_results = tile([P, 2, M], F32, "last_results", after="old_sb3")
+        add_and_store(2, last_results[:, 0, :], pieces=2)
+        add_and_store(3, last_results[:, 1, :], pieces=2)

@@ -24,9 +24,12 @@ def tile_attend_keylarger_written_lean_kernel(tc, query, keys, notes, slot_facto
     nc = tc.nc
     with ExitStack() as ctx:
         sb = ctx.enter_context(tc.tile_pool(name="sb", bufs=1))
+        shared = ctx.enter_context(tc.tile_pool(name="shared", bufs=1))
         ps = ctx.enter_context(tc.psum_pool(name="ps", bufs=1))
 
         def tile(shape, dtype, name, after=None):
+            if isinstance(after, int):
+                return shared.tile(shape, dtype, name=name, align_bytes=64, offset=after)
             return sb.tile(shape, dtype, name=name, tag=after or name, align_bytes=64)
 
         key_list = tile([P, I // 16], U16, "key_list")
@@ -37,7 +40,7 @@ def tile_attend_keylarger_written_lean_kernel(tc, query, keys, notes, slot_facto
         key_pool = [tile([P, T], F32, "key_pool%d" % j) for j in range(PACK)]
         note_pool = [tile([P, U], F32, "note_pool%d" % j) for j in range(PACK)]
         val_pool = [tile([P, T], F32, "val_pool%d" % k) for k in range(4)]
-        old_sb = [tile([P, M], F32, "old_sb%d" % k) for k in range(4)]
+        old_sb = [tile([P, M], F32, "old_sb%d" % k, after=3072 if k == 2 else None) for k in range(4)]
         query_sb = tile([P, PACK, Q], F32, "query_sb")
         factor_sb = tile([P, PACK], F32, "factor_sb")
         fade_sb = tile([P, 2, PACK], F32, "fade_sb")
@@ -90,12 +93,12 @@ def tile_attend_keylarger_written_lean_kernel(tc, query, keys, notes, slot_facto
         for k in range(4):
             nc.vector.memset(placed[k][:], 0.0)
 
-        zk_rows = tile([P, PACK, I], BF16, "zk_rows")
-        zk_places = zk_rows[:].rearrange("p j (t m) -> p j m t", t=PACK)
+        zk_pairs = tile([P, 2, I, 2], BF16, "zk_pairs")
+        zk_places = zk_pairs[:].rearrange("p g (t m) e -> p g e m t", t=PACK)
 
         def larger(j, slots, key_got, note_got):
             nc.vector.tensor_tensor(
-                zk_places[:, j, slots.start // PACK:slots.stop // PACK, :],
+                zk_places[:, j // 2, j % 2, slots.start // PACK:slots.stop // PACK, :],
                 key_got.rearrange("p (m t) -> p m t", t=PACK),
                 note_got.rearrange("p (m t) -> p m t", t=PACK),
                 ALU.max,
@@ -152,11 +155,12 @@ def tile_attend_keylarger_written_lean_kernel(tc, query, keys, notes, slot_facto
                         stop=True,
                     )
 
+        zk_words = zk_pairs[:].rearrange("p g c e -> p g (c e)").bitcast(F32)
         for g in range(2):
             cols = slice(2 * P * g, 2 * P * (g + 1))
             nc.vector.tensor_copy(
-                zk_bf[:, cols, :].rearrange("p (c i) j -> p c j i", i=4),
-                zk_rows[:, :, cols].rearrange("p j (c i) -> p c j i", i=4),
+                zk_bf[:, cols, :].bitcast(F32).rearrange("p (c i) g -> p c g i", i=4),
+                zk_words[:, :, cols].rearrange("p g (c i) -> p c g i", i=4),
             )
         quantize(query_codes, query_scales, query_bf[:])
         score(0)
@@ -250,12 +254,12 @@ def tile_attend_keylarger_written_lean_kernel(tc, query, keys, notes, slot_facto
         add_and_store(0, tile([P, M], F32, "result0", after="val_pool2"))
         turn_vals(2, True, None)
         quantize_vals(2, None)
-        read_vals(2, False, "val_pool3")
-        place(2)
         fade_old(2, None)
-        turn_vals(3, True, "old_sb2")
+        turn_vals(3, True, 3072)
+        read_vals(2, True, 6144)
+        place(2)
         quantize_vals(3, None)
-        add_and_store(1, tile([P, M], F32, "result1", after="old_sb2"))
+        add_and_store(1, tile([P, M], F32, "result1", after=0))
         read_vals(3, True, None)
         place(3)
         fade_old(3, "val_bf0")

from contextlib import ExitStack

import concourse.mybir as mybir
from concourse.masks import make_identity

D, T, I, Q, E, U, M = 512, 2048, 512, 256, 512, 1024, 1024
FLOPS = 2 * D * I * Q + 2 * I * E * Q

F32 = mybir.dt.float32
BF16 = mybir.dt.bfloat16
U32 = mybir.dt.uint32
U16 = mybir.dt.uint16
U8 = mybir.dt.uint8
FP8X4 = mybir.dt.float8_e4m3fn_x4
ALU = mybir.AluOpType
ACT = mybir.ActivationFunctionType

P = 128
PACK = 4
BANK = 512


def tile_attend_keylarger_written_lean_kernel(tc, query, keys, notes, slot_factor, vals, old, fade, offs, offs2, offs3, out):
    nc = tc.nc
    with ExitStack() as ctx:
        sb = ctx.enter_context(tc.tile_pool(name="sb", bufs=1))
        shared = ctx.enter_context(tc.tile_pool(name="shared", bufs=1))
        ps = ctx.enter_context(tc.psum_pool(name="ps", bufs=1))

        def tile(shape, dtype, name, after=None):
            if isinstance(after, int):
                return shared.tile(shape, dtype, name=name, align_bytes=64, offset=after)
            return sb.tile(shape, dtype, name=name, tag=after or name, align_bytes=64)

        key_list = tile([P, I // 16], U16, "key_list")
        note_list = tile([P, I // 16], U16, "note_list")
        place_list = tile([P, Q // 16], U16, "place_list")
        key_rows = keys.rearrange("(p j) t -> p j t", j=PACK)
        note_rows = notes.rearrange("(p j) u -> p j u", j=PACK)
        key_pool = [tile([P, T], F32, "key_pool%d" % j) for j in range(PACK)]
        note_pool = [tile([P, U], F32, "note_pool%d" % j) for j in range(PACK)]
        val_pool = [tile([P, T], F32, "val_pool%d" % k) for k in range(4)]
        old_sb = [tile([P, M], F32, "old_sb%d" % k, after=3072 if k == 2 else None) for k in range(4)]
        query_sb = tile([P, PACK, Q], F32, "query_sb")
        factor_sb = tile([P, PACK], F32, "factor_sb")
        fade_sb = tile([P, 2, PACK], F32, "fade_sb")

        def load_vals(k):
            nc.sync.dma_start(out=val_pool[k][:], in_=vals[k * P:(k + 1) * P, :])

        def load_old(k):
            nc.sync.dma_start(out=old_sb[k][:], in_=old[k * P:(k + 1) * P, :])

        nc.sync.dma_start(out=key_pool[0][:], in_=key_rows[:, 0, :])
        nc.sync.dma_start(key_list[:], offs)
        nc.sync.dma_start(note_list[:], offs2)
        nc.sync.dma_start(out=note_pool[0][:], in_=note_rows[:, 0, :])
        nc.scalar.dma_start(out=factor_sb[:], in_=slot_factor.rearrange("o (p t) -> p (o t)", t=PACK))
        nc.scalar.dma_start(out=fade_sb[:], in_=fade.rearrange("o (h p c) -> p (o h) c", h=2, c=PACK))
        for j in range(1, PACK):
            nc.sync.dma_start(out=key_pool[j][:], in_=key_rows[:, j, :])
            nc.sync.dma_start(out=note_pool[j][:], in_=note_rows[:, j, :])
        nc.sync.dma_start(out=query_sb[:], in_=query.rearrange("(p j) q -> p j q", j=PACK))
        load_vals(0)
        load_old(0)
        load_vals(1)
        nc.sync.dma_start(place_list[:], offs3)
        load_old(1)
        load_vals(2)
        load_vals(3)
        load_old(2)
        load_old(3)

        zero = tile([P, 1], F32, "zero")
        unread = tile([P, 1], F32, "unread")
        nc.vector.memset(zero[:], 0.0)
        nc.scalar.activation(unread[:], zero[:], ACT.Sigmoid)

        ident = tile([P, P], F32, "ident")
        make_identity(nc, ident[:])

        fade_all = tile([P, M], F32, "fade_all")
        for h in range(2):
            fade_bank = ps.tile([P, PACK, P], F32, name="fade_bank%d" % h)
            for c in range(PACK):
                nc.tensor.transpose(fade_bank[:, c, :], fade_sb[:, h, c:c + 1].to_broadcast([P, P]), ident[:])
            nc.scalar.copy(
                out=fade_all[:, h * BANK:(h + 1) * BANK].rearrange("p (n c) -> p n c", c=PACK),
                in_=fade_bank[:].rearrange("p c n -> p n c"),
            )

        placed = [tile([P, M], F32, "placed%d" % k) for k in range(4)]
        for k in range(4):
            nc.vector.memset(placed[k][:], 0.0)

        zk_pairs = tile([P, 2, I, 2], BF16, "zk_pairs")
        zk_places = zk_pairs[:].rearrange("p g (t m) e -> p g e m t", t=PACK)

        def larger(j, slots, key_got, note_got):
            nc.vector.tensor_tensor(
                zk_places[:, j // 2, j % 2, slots.start // PACK:slots.stop // PACK, :],
                key_got.rearrange("p (m t) -> p m t", t=PACK),
                note_got.rearrange("p (m t) -> p m t", t=PACK),
                ALU.max,
            )

        last = PACK - 1
        half = I // 2
        for j in range(last):
            key_got = tile([P, I], F32, "key_got%d" % j)
            note_got = tile([P, I], F32, "note_got%d" % j)
            nc.scalar.activation(key_got[:], key_pool[j][:].indirect(key_list[:]), ACT.Copy)
            nc.vector.tensor_copy(note_got[:], note_pool[j][:].indirect(note_list[:]))
            larger(j, slice(0, I), key_got[:], note_got[:])
        key_got = tile([P, I], F32, "key_got3")
        nc.scalar.activation(key_got[:], key_pool[last][:].indirect(key_list[:]), ACT.Copy)
        note_low = tile([P, half], F32, "note_low")
        note_high = tile([P, half], F32, "note_high", after="key_pool3")
        nc.vector.tensor_copy(note_low[:], note_pool[last][:].indirect(note_list[:, :half // 16]))
        nc.scalar.activation(note_high[:], note_pool[last][:].indirect(note_list[:, half // 16:]), ACT.Copy)
        larger(last, slice(0, half), key_got[:, :half], note_low[:])
        larger(last, slice(half, I), key_got[:, half:], note_high[:])

        query_bf = tile([P, Q, PACK], BF16, "query_bf", after="note_pool3")
        nc.scalar.copy(
            out=query_bf[:].rearrange("p (c i) j -> p c j i", i=4),
            in_=query_sb[:].rearrange("p j (c i) -> p c j i", i=4),
        )
        query_codes = tile([P, Q], U32, "query_codes")
        query_scales = tile([P, Q], U8, "query_scales")

        zk_bf = tile([P, I, PACK], BF16, "zk_bf")
        zk_codes = [tile([P, 2 * P], U32, "zk_codes%d" % g, after=[None, "note_pool3"][g]) for g in range(2)]
        zk_scales = [tile([P, 2 * P], U8, "zk_scales%d" % g) for g in range(2)]
        scores = [ps.tile([P, PACK, P], F32, name="scores%d" % h) for h in range(2)]

        def quantize(codes, scales, values):
            nc.vector.quantize_mx(
                out=codes[:].bitcast(FP8X4), scales=scales[:], in_=values.rearrange("p c j -> p (c j)")
            )

        def score(g):
            quantize(zk_codes[g], zk_scales[g], zk_bf[:, 2 * P * g:2 * P * (g + 1), :])
            for h in range(2):
                rows = slice(h * P, (h + 1) * P)
                for r in range(2):
                    slots = slice(r * P, (r + 1) * P)
                    nc.tensor.matmul_mx(
                        out=scores[h][:, 2 * g + r, :],
                        lhsT=zk_codes[g][:, slots].bitcast(FP8X4),
                        lhsT_scale=zk_scales[g][:, slots],
                        rhs=query_codes[:, rows].bitcast(FP8X4),
                        rhs_scale=query_scales[:, rows],
                        start=True,
                        stop=True,
                    )

        zk_words = zk_pairs[:].rearrange("p g c e -> p g (c e)").bitcast(F32)
        for g in range(2):
            cols = slice(2 * P * g, 2 * P * (g + 1))
            nc.vector.tensor_copy(
                zk_bf[:, cols, :].bitcast(F32).rearrange("p (c i) g -> p c g i", i=4),
                zk_words[:, :, cols].rearrange("p g (c i) -> p c g i", i=4),
            )
        quantize(query_codes, query_scales, query_bf[:])
        score(0)
        score(1)

        got, val_bf, val_codes, val_scales, read_sb, faded = {}, {}, {}, {}, {}, {}

        def gather_vals(k, on_vector, after):
            got[k] = tile([P, I], BF16, "val_got%d" % k, after=after)
            looked_up = val_pool[k][:].indirect(key_list[:])
            if on_vector:
                nc.vector.tensor_copy(got[k][:], looked_up)
            else:
                nc.scalar.activation(got[k][:], looked_up, ACT.Copy)

        def turn_vals(k, on_vector, after):
            words = got[k][:].bitcast(F32)
            turned = ps.tile([P, 2, P], F32, name="turned%d" % k, tag="turned%d" % (k % 2))
            for u in range(2):
                nc.tensor.transpose(turned[:, u, :], words[:, u:I // 2:2], ident[:])
            val_bf[k] = tile([P, P, PACK], BF16, "val_bf%d" % k, after=after)
            if on_vector:
                nc.vector.tensor_copy(val_bf[k][:].bitcast(F32), turned[:].rearrange("p u e -> p e u"))
            else:
                nc.scalar.copy(out=val_bf[k][:].bitcast(F32), in_=turned[:].rearrange("p u e -> p e u"))

        def quantize_vals(k, after):
            val_codes[k] = tile([P, P], U32, "val_codes%d" % k, after=after)
            val_scales[k] = tile([P, P], U8, "val_scales%d" % k)
            quantize(val_codes[k], val_scales[k], val_bf[k][:])

        weight_codes = tile([P, Q], U32, "weight_codes")
        weight_scales = tile([P, Q], U8, "weight_scales")

        def read_vals(k, on_vector, after):
            read = ps.tile([P, Q], F32, name="read%d" % k, tag="read%d" % (k % 2))
            nc.tensor.matmul_mx(
                out=read[:],
                lhsT=val_codes[k][:].bitcast(FP8X4),
                lhsT_scale=val_scales[k][:],
                rhs=weight_codes[:].bitcast(FP8X4),
                rhs_scale=weight_scales[:],
                start=True,
                stop=True,
            )
            read_sb[k] = tile([P, Q], F32, "read_sb%d" % k, after=after)
            if on_vector:
                nc.vector.tensor_copy(read_sb[k][:], read[:])
            else:
                nc.scalar.copy(out=read_sb[k][:], in_=read[:])

        def place(k):
            nc.scalar.activation(placed[k][:].indirect(place_list[:]), read_sb[k][:], ACT.Copy)

        def fade_old(k, after):
            faded[k] = tile([P, M], F32, "faded%d" % k, after=after)
            nc.vector.tensor_tensor(faded[k][:], old_sb[k][:], fade_all[:], ALU.mult)

        def add_and_store(k, result, pieces=1):
            for n in range(pieces):
                cols = slice(n * M // pieces, (n + 1) * M // pieces)
                nc.vector.tensor_tensor(result[:, cols], faded[k][:, cols], placed[k][:, cols], ALU.add)
                nc.sync.dma_start(out=out[k * P:(k + 1) * P, cols], in_=result[:, cols])

        gather_vals(0, False, "query_sb")
        fade_old(0, "zk_bf")
        weight_bf = tile([P, Q, PACK], BF16, "weight_bf", after="old_sb0")
        weight = tile([P, Q, PACK], F32, "weight", after="val_pool0")
        for h in range(2):
            rows = slice(h * P, (h + 1) * P)
            nc.scalar.activation(weight[:, rows, :], scores[h][:].rearrange("p t q -> p q t"), ACT.Sigmoid)
            nc.vector.tensor_tensor(
                weight_bf[:, rows, :],
                weight[:, rows, :],
                factor_sb[:].unsqueeze(1).to_broadcast([P, P, PACK]),
                ALU.mult,
            )
        turn_vals(0, False, None)
        quantize_vals(0, "val_pool0")
        quantize(weight_codes, weight_scales, weight_bf[:])
        gather_vals(1, False, "query_sb")
        read_vals(0, False, "val_pool1")
        place(0)
        fade_old(1, "val_bf0")
        turn_vals(1, True, "old_sb1")
        quantize_vals(1, None)
        gather_vals(2, True, None)
        gather_vals(3, False, "val_pool1")
        read_vals(1, False, "val_pool3")
        place(1)
        add_and_store(0, tile([P, M], F32, "result0", after="val_pool2"))
        turn_vals(2, True, None)
        quantize_vals(2, None)
        fade_old(2, None)
        turn_vals(3, True, 3072)
        read_vals(2, True, 6144)
        place(2)
        quantize_vals(3, None)
        add_and_store(1, tile([P, M], F32, "result1", after=0))
        read_vals(3, True, None)
        place(3)
        fade_old(3, "val_bf0")
        last_results = tile([P, 2, M], F32, "last_results", after="old_sb3")
        add_and_store(2, last_results[:, 0, :], pieces=2)
        add_and_store(3, last_results[:, 1, :], pieces=2)
